import numpy as np
import ml_dtypes


def mxq(x, axis, fmt="e4m3"):
    dtype, down = {"e4m3": (ml_dtypes.float8_e4m3fn, 7), "e5m2": (ml_dtypes.float8_e5m2, 14)}[fmt]
    v = np.moveaxis(np.asarray(x, np.float32).astype(ml_dtypes.bfloat16).astype(np.float64), axis, -1)
    blocks = v.reshape(v.shape[:-1] + (-1, 32))
    amax = np.abs(blocks).max(-1, keepdims=True)
    byte = np.maximum(np.where(amax > 0, np.frexp(amax)[1] - 1 + 127, 0) - down, 1)
    scale = np.exp2(byte - 127.0)
    codes = (blocks / scale).astype(np.float32).astype(dtype).astype(np.float64)
    return np.moveaxis((codes * scale).reshape(v.shape), -1, axis)


WIDE = False


def mx_kscale(k):
    if not WIDE:
        return np.ones(k)
    levels = np.array([30, -30])
    if k % 512:
        return np.exp2(np.random.permutation(np.resize(levels, k // 32))).repeat(32)
    a = np.empty((k // 512, 16))
    for p in range(k // 512):
        a[p, :8] = np.random.permutation(np.resize(levels, 8))
        for g in range(8):
            far = levels[np.abs(levels - a[p, g]) >= 10]
            a[p, g + 8] = far[np.random.randint(len(far))]
    return np.exp2(a.ravel()).repeat(32)


def f64(x):
    return np.asarray(x).astype(np.float64)


def striped(idx):
    return np.tile(np.asarray(idx).reshape(-1, 16).T, (8, 1)).astype(np.uint16)


def unstriped(offs):
    return offs[:16].T.reshape(-1).astype(np.int64)


def striped8(idx):
    return np.asarray(idx).reshape(8, -1, 16).transpose(0, 2, 1).reshape(128, -1).astype(np.uint16)


def unstriped8(offs):
    return offs.reshape(8, 16, -1).transpose(0, 2, 1).reshape(8, -1).astype(np.int64)


def pick8(x, idx, run):
    r = np.arange(len(x))
    return x[r[:, None], idx[r % (8 * run) // run]]


E2M1 = np.array([0.0, 0.5, 1.0, 1.5, 2.0, 3.0, 4.0, 6.0, -0.0, -0.5, -1.0, -1.5, -2.0, -3.0, -4.0, -6.0])


def pack_weight(w, fmt):
    k, n = w.shape
    w = f64(np.asarray(w, np.float32).astype(ml_dtypes.bfloat16)).reshape(k // 32, 32, n)
    amax = np.abs(w).max(1)
    if fmt in ("e4m3", "e5m2"):
        byte = np.frexp(amax)[1] - 1 + 127 - (7 if fmt == "e4m3" else 14)
    else:
        mant, ex = np.frexp(amax / 6.0)
        byte = np.where(mant > 0.5, ex, ex - 1) + 127
    byte = np.clip(np.where(amax > 0, byte, 1), 1, 254)
    scaled = (w * np.exp2(127.0 - byte)[:, None, :]).reshape(k, n).astype(np.float32)
    by_word = np.ascontiguousarray(scaled.reshape(k // 512, 128, 4, n).transpose(0, 1, 3, 2))
    if fmt in ("e4m3", "e5m2"):
        words = by_word.astype(ml_dtypes.float8_e4m3fn if fmt == "e4m3" else ml_dtypes.float8_e5m2).view(np.uint8)
    else:
        c = by_word.astype(ml_dtypes.float4_e2m1fn).view(np.uint8) & 0xF
        words = (c[..., 0::2] | (c[..., 1::2] << 4)).reshape(k // 512, 128, 2 * n)
    return np.ascontiguousarray(words), np.ascontiguousarray(byte.astype(np.uint8).reshape(k // 512, 16, n))


def unpack_weight(words, scales, fmt):
    g, _, n = scales.shape
    words = np.ascontiguousarray(words).reshape(g, 128, n, -1)
    if fmt in ("e4m3", "e5m2"):
        vals = words.view(ml_dtypes.float8_e4m3fn if fmt == "e4m3" else ml_dtypes.float8_e5m2).astype(np.float64)
    else:
        nib = np.empty((g, 128, n, 4), np.uint8)
        nib[..., 0::2] = words & 0xF
        nib[..., 1::2] = words >> 4
        vals = E2M1[nib]
    vals = vals * np.repeat(np.exp2(scales.astype(np.float64) - 127.0), 8, axis=1)[..., None]
    return vals.transpose(0, 1, 3, 2).reshape(g * 512, n)


K, T, J, R, F, Z, C, O, N = 512, 1024, 256, 512, 512, 1024, 512, 128, 256


def setup_inputs():
    n = np.random.standard_normal
    idx = np.random.permutation(T)[:J]
    idx2 = np.random.permutation(Z)[:J]
    idx3 = np.stack([np.random.permutation(C)[:J] for _ in range(8)])
    idx4 = np.stack([np.random.permutation(C)[:J] for _ in range(8)])
    idx5 = np.random.permutation(C)[:O]
    idx6 = np.random.permutation(C)[:O]
    idx7 = np.random.permutation(T)[:O]
    fk = mx_kscale(K)
    ff = mx_kscale(F)
    fr = mx_kscale(R)
    xtp = pack_weight(n((K, T)) / fk[:, None], "e4m3")
    xop = pack_weight(n((F, Z)) / ff[:, None], "e2m1")
    wp = pack_weight(n((K, R)) * 1 / np.sqrt(K) * fk[:, None] * fr, "e2m1")
    w2p = pack_weight(n((F, R)) * 1 / np.sqrt(F) * ff[:, None] * fr, "e5m2")
    wbp = pack_weight(n((R, N)) * 1 / np.sqrt(R) / fr[:, None], "e5m2")
    wsp = pack_weight(n((K, N)) * 1 / np.sqrt(K) * fk[:, None], "e5m2")
    return {
        "xt_words": xtp[0],
        "xt_scales": xtp[1],
        "xo_words": xop[0],
        "xo_scales": xop[1],
        "w_words": wp[0],
        "w_scales": wp[1],
        "w2_words": w2p[0],
        "w2_scales": w2p[1],
        "sa": (np.random.uniform(0.5, 1.6, (R, 1))).astype(np.float32),
        "sb": (np.random.uniform(0.5, 1.6, (R, 1))).astype(np.float32),
        "wb_words": wbp[0],
        "wb_scales": wbp[1],
        "ws_words": wsp[0],
        "ws_scales": wsp[1],
        "offs": striped(idx),
        "offs2": striped(idx2),
        "offs3": striped8(idx3),
        "offs4": striped8(idx4),
        "offs5": striped(idx5),
        "offs6": striped(idx6),
        "offs7": striped(idx7),
    }


def reference(xt_words, xt_scales, xo_words, xo_scales, w_words, w_scales, w2_words, w2_scales, sa, sb, wb_words, wb_scales, ws_words, ws_scales, offs, offs2, offs3, offs4, offs5, offs6, offs7):
    idx = unstriped(offs)
    idx2 = unstriped(offs2)
    idx3 = unstriped8(offs3)
    idx4 = unstriped8(offs4)
    idx5 = unstriped(offs5)
    idx6 = unstriped(offs6)
    idx7 = unstriped(offs7)
    xtu = unpack_weight(xt_words, xt_scales, "e4m3")
    xou = unpack_weight(xo_words, xo_scales, "e2m1")
    wu = unpack_weight(w_words, w_scales, "e2m1")
    w2u = unpack_weight(w2_words, w2_scales, "e5m2")
    wbu = unpack_weight(wb_words, wb_scales, "e5m2")
    wsu = unpack_weight(ws_words, ws_scales, "e5m2")
    xtidxg = xtu[:, idx]
    a = wu.T @ xtidxg
    xoidx2g = xou[:, idx2]
    b = w2u.T @ xoidx2g
    pw = np.zeros((R, C))
    pw[np.arange(R)[:, None], idx3[np.arange(R) % 512 // 64]] = a
    pv = np.zeros((R, C))
    pv[np.arange(R)[:, None], idx4[np.arange(R) % 512 // 64]] = b
    pg = pw + pv
    hid = np.abs(pg[:, idx5] * f64(sa) - pg[:, idx6] * f64(sb))
    hidq = mxq(hid, 0, "e4m3")
    xtidx7g = xtu[:, idx7]
    y = wbu.T @ hidq + wsu.T @ xtidx7g
    return y

@@ -1,0 +1,202 @@
+from contextlib import ExitStack
+
+import concourse.mybir as mybir
+
+K, T, J, R, Z, C, O, N = 512, 1024, 256, 512, 1024, 512, 128, 256
+FLOPS = 2 * K * (2 * R * J + 2 * N * O)
+
+F32 = mybir.dt.float32
+BF16 = mybir.dt.bfloat16
+I32 = mybir.dt.int32
+U32 = mybir.dt.uint32
+U16 = mybir.dt.uint16
+U8 = mybir.dt.uint8
+E4M3 = mybir.dt.float8_e4m3fn_x4
+E5M2 = mybir.dt.float8_e5m2_x4
+E2M1 = mybir.dt.float4_e2m1fn_x4
+COPY = mybir.ActivationFunctionType.Copy
+ALU = mybir.AluOpType
+
+P = 128
+PACK = 4
+QUADS = 4
+QUAD = 32
+LANES = 16
+
+
+def tile_list_ownsum_twotab_further_plain_kernel(
+    tc, xt_words, xt_scales, xo_words, xo_scales, w_words, w_scales, w2_words, w2_scales, sa, sb,
+    wb_words, wb_scales, ws_words, ws_scales, offs, offs2, offs3, offs4, offs5, offs6, offs7, out,
+):
+    nc = tc.nc
+    with ExitStack() as ctx:
+        pool = ctx.enter_context(tc.tile_pool(name="keep", bufs=1))
+        psum = ctx.enter_context(tc.psum_pool(name="psum", bufs=1))
+
+        def sbuf(name, cols, dtype, tag=None):
+            return pool.tile([P, cols], dtype, name=name, tag=tag or name, align_bytes=64)
+
+        def load_list(name, src):
+            t = pool.tile([P, src.shape[1]], U16, name=name)
+            nc.sync.dma_start(t[:], src)
+            return t
+
+        def load_words(name, src, dtype):
+            rows = src[0] if src.ndim == 3 else src[0].rearrange("p n t -> p (n t)")
+            rows = rows.bitcast(I32)
+            t = sbuf(name, rows.shape[1] * (2 if dtype == U16 else 1), dtype)
+            nc.sync.dma_start(t[:].bitcast(I32), rows)
+            return t
+
+        def load_scales(name, src):
+            plane = sbuf(name, src.shape[2], U8)
+            for q in range(QUADS):
+                rows = src[0, PACK * q : PACK * (q + 1), :].bitcast(I32)
+                nc.sync.dma_start(
+                    plane[QUAD * q : QUAD * (q + 1), :].bitcast(I32), rows.partition_broadcast(QUAD // PACK)
+                )
+            return plane
+
+        def deal(dst, src, t0, t1):
+            nc.vector.tensor_copy(
+                dst[:].rearrange("p (t m) -> p t m", t=PACK)[:, t0:t1, :],
+                src[:].rearrange("p (m t) -> p t m", t=PACK)[:, t0:t1, :],
+            )
+
+        def entries(lst, j0, j1):
+            return lst[:, j0 // LANES : j1 // LANES]
+
+        l2 = load_list("l2", offs2)
+        w2_stage = pool.tile([PACK, QUADS, R // 4], I32, name="w2_stage", tag="w2_stage", align_bytes=64)
+        nc.sync.dma_start(w2_stage[:], w2_scales[0].bitcast(I32).rearrange("(q r) n -> r q n", r=PACK))
+        xo_s = load_scales("xo_s", xo_scales)
+        xo_w = load_words("xo_w", xo_words, U16)
+        w2_w = load_words("w2_w", w2_words, U32)
+        l4 = load_list("l4", offs4)
+        l1 = load_list("l1", offs)
+        xt_w = load_words("xt_w", xt_words, U32)
+        xt_s = load_scales("xt_s", xt_scales)
+        w_w = load_words("w_w", w_words, U16)
+        w_s = load_scales("w_s", w_scales)
+        l3 = load_list("l3", offs3)
+        l7 = load_list("l7", offs7)
+        l5 = load_list("l5", offs5)
+        l6 = load_list("l6", offs6)
+        sa_t = pool.tile([P, PACK], F32, name="sa_t")
+        sb_t = pool.tile([P, PACK], F32, name="sb_t")
+        nc.sync.dma_start(sa_t[:], sa.rearrange("(p t) o -> p (t o)", t=PACK))
+        nc.sync.dma_start(sb_t[:], sb.rearrange("(p t) o -> p (t o)", t=PACK))
+        ws_w = load_words("ws_w", ws_words, U32)
+        ws_s = load_scales("ws_s", ws_scales)
+        wb_w = load_words("wb_w", wb_words, U32)
+        wb_s = load_scales("wb_s", wb_scales)
+
+        w2_s = sbuf("w2_s", R, U8)
+        nc.vector.memset(w2_s[:].bitcast(I32), 0)
+        pv = [sbuf("pv%d" % t, C, F32) for t in range(PACK)]
+        pw = [sbuf("pw0", C, F32)]
+        for board in pv[:2]:
+            nc.vector.memset(board[:], 0.0)
+        for board in pv[2:] + pw:
+            nc.gpsimd.memset(board[:], 0.0)
+
+        def product(res, t, j0, j1, wd, sd, wfmt, gw, gs, gfmt, on_scalar):
+            cols = slice(P * t, P * (t + 1))
+            acc = psum.tile([P, j1 - j0], F32, name="acc", tag="acc", bufs=6)
+            nc.tensor.matmul_mx(
+                acc[:], lhsT=wd[:, cols].bitcast(wfmt), lhsT_scale=sd[:, cols],
+                rhs=gw[:, j0:j1].bitcast(gfmt), rhs_scale=gs[:, j0:j1], start=True, stop=True,
+            )
+            if on_scalar:
+                nc.scalar.activation(res[:, j0:j1], acc[:], COPY)
+            else:
+                nc.vector.tensor_copy(res[:, j0:j1], acc[:])
+
+        w2_sd = sbuf("w2_sd", R, U8)
+        w2_wd = sbuf("w2_wd", R, U32)
+        xo_gs = sbuf("xo_gs", J, U8)
+        xo_gw = sbuf("xo_gw", J, U16)
+        b = [sbuf("b%d" % t, J, F32) for t in range(PACK)]
+        for q in range(QUADS):
+            nc.vector.tensor_copy(w2_s[QUAD * q : QUAD * q + PACK, :].bitcast(I32), w2_stage[:, q, :])
+        deal(w2_sd, w2_s, 0, PACK)
+        half = J // 2
+        for piece, j0 in enumerate((0, half)):
+            j1 = j0 + half
+            nc.vector.tensor_copy(xo_gs[:, j0:j1], xo_s[:].indirect(entries(l2, j0, j1)))
+            nc.vector.tensor_copy(xo_gw[:, j0:j1], xo_w[:].indirect(entries(l2, j0, j1)))
+            deal(w2_wd, w2_w, piece, piece + 1)
+            product(b[0], 0, j0, j1, w2_wd, w2_sd, E5M2, xo_gw, xo_gs, E2M1, piece == 0)
+            nc.scalar.activation(pv[0][:].indirect(entries(l4, j0, j1)), b[0][:, j0:j1], COPY)
+        for t in range(1, PACK):
+            if t == 2:
+                deal(w2_wd, w2_w, 2, PACK)
+            product(b[t], t, 0, J, w2_wd, w2_sd, E5M2, xo_gw, xo_gs, E2M1, False)
+            nc.scalar.activation(pv[t][:].indirect(l4[:]), b[t][:], COPY)
+
+        pw.append(sbuf("pw1", C, F32, tag="w2_w"))
+        nc.vector.memset(pw[1][:], 0.0)
+        w_sd = sbuf("w_sd", R, U8, tag="w2_sd")
+        w_wd = sbuf("w_wd", R, U16, tag="w2_wd")
+        xt_gs = sbuf("xt_gs", J, U8, tag="xo_gs")
+        xt_gw = sbuf("xt_gw", J, U32, tag="xo_gw")
+        nc.vector.tensor_copy(xt_gs[:], xt_s[:].indirect(l1[:]))
+        nc.vector.tensor_copy(xt_gw[:], xt_w[:].indirect(l1[:]))
+        deal(w_sd, w_s, 0, PACK)
+        deal(w_wd, w_w, 0, PACK)
+        a = [sbuf("a%d" % t, J, F32) for t in range(PACK)]
+        for t in range(PACK):
+            product(a[t], t, 0, J, w_wd, w_sd, E2M1, xt_gw, xt_gs, E4M3, False)
+
+        x7_gs = sbuf("x7_gs", O, U8, tag="xo_gs")
+        x7_gw = sbuf("x7_gw", O, U32, tag="xo_gw")
+        nc.vector.tensor_copy(x7_gs[:], xt_s[:].indirect(l7[:]))
+        nc.vector.tensor_copy(x7_gw[:], xt_w[:].indirect(l7[:]))
+        halves = N // P
+        y = [psum.tile([P, O], F32, name="y%d" % h) for h in range(halves)]
+        for h in range(halves):
+            cols = slice(P * h, P * (h + 1))
+            nc.tensor.matmul_mx(
+                y[h][:], lhsT=ws_w[:, cols].bitcast(E5M2), lhsT_scale=ws_s[:, cols],
+                rhs=x7_gw[:].bitcast(E4M3), rhs_scale=x7_gs[:], start=True, stop=False,
+            )
+
+        pg = [sbuf("pg%d" % t, C, F32) for t in range(PACK)]
+        hid = pool.tile([P, O, PACK], BF16, name="hid", align_bytes=64)
+        clocks = {}
+
+        def put_a(t):
+            nc.scalar.activation(pw[t % 2][:].indirect(l3[:]), a[t][:], COPY)
+            nc.vector.tensor_tensor(pg[t][:], pw[t % 2][:], pv[t][:], ALU.add)
+
+        def fetch(t):
+            ga = sbuf("ga%d" % t, O, F32)
+            gb = sbuf("gb%d" % t, O, F32)
+            nc.scalar.activation(ga[:], pg[t][:].indirect(l5[:]), COPY, scale=sa_t[:, t : t + 1])
+            nc.scalar.activation(gb[:], pg[t][:].indirect(l6[:]), COPY, scale=sb_t[:, t : t + 1])
+            d = sbuf("d%d" % t, O, F32)
+            nc.vector.tensor_tensor(d[:], ga[:], gb[:], ALU.subtract)
+            nc.vector.scalar_tensor_tensor(hid[:, :, t], d[:], -1.0, d[:], ALU.mult, ALU.max)
+            clocks[t] = gb
+
+        put_a(0)
+        for t in range(1, PACK):
+            put_a(t)
+            fetch(t - 1)
+        fetch(PACK - 1)
+
+        hid_w = sbuf("hid_w", O, U32)
+        hid_s = sbuf("hid_s", O, U8)
+        nc.vector.quantize_mx(hid_w[:].bitcast(E4M3), hid_s[:], hid[:].rearrange("p o t -> p (o t)"))
+        for h in range(halves):
+            cols = slice(P * h, P * (h + 1))
+            nc.tensor.matmul_mx(
+                y[h][:], lhsT=wb_w[:, cols].bitcast(E5M2), lhsT_scale=wb_s[:, cols],
+                rhs=hid_w[:].bitcast(E4M3), rhs_scale=hid_s[:], start=False, stop=True,
+            )
+        y0 = sbuf("y0s", O, F32)
+        y1 = sbuf("y1s", O, F32)
+        nc.vector.tensor_copy(y0[:], y[0][:])
+        nc.sync.dma_start(out[0:P, :], y0[:])
+        nc.scalar.activation(y1[:], y[1][:], COPY)
+        nc.scalar.dma_start(out[P:N, :], y1[:])

@@ -31,10 +31,14 @@ def tile_list_ownsum_twotab_further_plain_kernel(
     nc = tc.nc
     with ExitStack() as ctx:
         pool = ctx.enter_context(tc.tile_pool(name="keep", bufs=1))
+        shared = ctx.enter_context(tc.tile_pool(name="shared", bufs=1))
         psum = ctx.enter_context(tc.psum_pool(name="psum", bufs=1))
 
         def sbuf(name, cols, dtype, tag=None):
             return pool.tile([P, cols], dtype, name=name, tag=tag or name, align_bytes=64)
+
+        def tenant(name, cols, dtype, offset):
+            return shared.tile([P, cols], dtype, name=name, align_bytes=64, offset=offset)
 
         def load_list(name, src):
             t = pool.tile([P, src.shape[1]], U16, name=name)
@@ -59,8 +63,8 @@ def tile_list_ownsum_twotab_further_plain_kernel(
 
         def deal(dst, src, t0, t1):
             nc.vector.tensor_copy(
-                dst[:].rearrange("p (t m) -> p t m", t=PACK)[:, t0:t1, :],
-                src[:].rearrange("p (m t) -> p t m", t=PACK)[:, t0:t1, :],
+                dst[:].rearrange("p (t m) -> p m t", m=P),
+                src[:].rearrange("p (m t) -> p m t", t=PACK)[:, :, t0:t1],
             )
 
         def entries(lst, j0, j1):
@@ -71,7 +75,8 @@ def tile_list_ownsum_twotab_further_plain_kernel(
         nc.sync.dma_start(w2_stage[:], w2_scales[0].bitcast(I32).rearrange("(q r) n -> r q n", r=PACK))
         xo_s = load_scales("xo_s", xo_scales)
         xo_w = load_words("xo_w", xo_words, U16)
-        w2_w = load_words("w2_w", w2_words, U32)
+        w2_w = tenant("w2_w", R, U32, 0)
+        nc.sync.dma_start(w2_w[:].bitcast(I32), w2_words[0].rearrange("p n t -> p (n t)").bitcast(I32))
         l4 = load_list("l4", offs4)
         l1 = load_list("l1", offs)
         xt_w = load_words("xt_w", xt_words, U32)
@@ -100,56 +105,71 @@ def tile_list_ownsum_twotab_further_plain_kernel(
         for board in pv[2:] + pw:
             nc.gpsimd.memset(board[:], 0.0)
 
-        def product(res, t, j0, j1, wd, sd, wfmt, gw, gs, gfmt, on_scalar):
-            cols = slice(P * t, P * (t + 1))
-            acc = psum.tile([P, j1 - j0], F32, name="acc", tag="acc", bufs=6)
+        def product(acc, words, scales, wfmt, gw, gs, gfmt):
             nc.tensor.matmul_mx(
-                acc[:], lhsT=wd[:, cols].bitcast(wfmt), lhsT_scale=sd[:, cols],
-                rhs=gw[:, j0:j1].bitcast(gfmt), rhs_scale=gs[:, j0:j1], start=True, stop=True,
+                acc, lhsT=words.bitcast(wfmt), lhsT_scale=scales,
+                rhs=gw[:].bitcast(gfmt), rhs_scale=gs[:], start=True, stop=True,
             )
-            if on_scalar:
-                nc.scalar.activation(res[:, j0:j1], acc[:], COPY)
-            else:
-                nc.vector.tensor_copy(res[:, j0:j1], acc[:])
 
-        w2_sd = sbuf("w2_sd", R, U8)
+        def bank(cols):
+            return psum.tile([P, cols], F32, name="acc", tag="acc", bufs=6)
+
+        half = J // 2
         w2_wd = sbuf("w2_wd", R, U32)
-        xo_gs = sbuf("xo_gs", J, U8)
-        xo_gw = sbuf("xo_gw", J, U16)
+        w2_sd0 = sbuf("w2_sd0", P, U8)
         b = [sbuf("b%d" % t, J, F32) for t in range(PACK)]
         for q in range(QUADS):
             nc.vector.tensor_copy(w2_s[QUAD * q : QUAD * q + PACK, :].bitcast(I32), w2_stage[:, q, :])
-        deal(w2_sd, w2_s, 0, PACK)
-        half = J // 2
-        for piece, j0 in enumerate((0, half)):
-            j1 = j0 + half
-            nc.vector.tensor_copy(xo_gs[:, j0:j1], xo_s[:].indirect(entries(l2, j0, j1)))
-            nc.vector.tensor_copy(xo_gw[:, j0:j1], xo_w[:].indirect(entries(l2, j0, j1)))
-            deal(w2_wd, w2_w, piece, piece + 1)
-            product(b[0], 0, j0, j1, w2_wd, w2_sd, E5M2, xo_gw, xo_gs, E2M1, piece == 0)
-            nc.scalar.activation(pv[0][:].indirect(entries(l4, j0, j1)), b[0][:, j0:j1], COPY)
+        xo_gs = [sbuf("xo_gs0", half, U8)]
+        xo_gw = [sbuf("xo_gw0", half, U16)]
+        nc.vector.tensor_copy(xo_gs[0][:], xo_s[:].indirect(entries(l2, 0, half)))
+        deal(w2_sd0, w2_s, 0, 1)
+        nc.vector.tensor_copy(xo_gw[0][:], xo_w[:].indirect(entries(l2, 0, half)))
+        deal(w2_wd, w2_w, 0, PACK)
+        acc = bank(half)
+        product(acc[:], w2_wd[:, 0:P], w2_sd0[:], E5M2, xo_gw[0], xo_gs[0], E2M1)
+        nc.scalar.activation(b[0][:, 0:half], acc[:], COPY)
+        nc.scalar.activation(pv[0][:].indirect(entries(l4, 0, half)), b[0][:, 0:half], COPY)
+
+        xo_gs.append(tenant("xo_gs1", half, U8, 0))
+        xo_gw.append(tenant("xo_gw1", half, U16, half))
+        w2_sdr = tenant("w2_sdr", R - P, U8, 3 * half)
+        nc.vector.tensor_copy(xo_gs[1][:], xo_s[:].indirect(entries(l2, half, J)))
+        nc.vector.tensor_copy(xo_gw[1][:], xo_w[:].indirect(entries(l2, half, J)))
+        acc = bank(half)
+        product(acc[:], w2_wd[:, 0:P], w2_sd0[:], E5M2, xo_gw[1], xo_gs[1], E2M1)
+        nc.vector.tensor_copy(b[0][:, half:J], acc[:])
+        nc.scalar.activation(pv[0][:].indirect(entries(l4, half, J)), b[0][:, half:J], COPY)
+        deal(w2_sdr, w2_s, 1, PACK)
         for t in range(1, PACK):
-            if t == 2:
-                deal(w2_wd, w2_w, 2, PACK)
-            product(b[t], t, 0, J, w2_wd, w2_sd, E5M2, xo_gw, xo_gs, E2M1, False)
+            acc = bank(J)
+            for i in range(2):
+                product(
+                    acc[:, half * i : half * (i + 1)], w2_wd[:, P * t : P * (t + 1)],
+                    w2_sdr[:, P * (t - 1) : P * t], E5M2, xo_gw[i], xo_gs[i], E2M1,
+                )
+            nc.vector.tensor_copy(b[t][:], acc[:])
             nc.scalar.activation(pv[t][:].indirect(l4[:]), b[t][:], COPY)
 
-        pw.append(sbuf("pw1", C, F32, tag="w2_w"))
+        pw.append(sbuf("pw1", C, F32, tag="xo_w"))
         nc.vector.memset(pw[1][:], 0.0)
-        w_sd = sbuf("w_sd", R, U8, tag="w2_sd")
+        w_sd = tenant("w_sd", R, U8, 0)
         w_wd = sbuf("w_wd", R, U16, tag="w2_wd")
-        xt_gs = sbuf("xt_gs", J, U8, tag="xo_gs")
-        xt_gw = sbuf("xt_gw", J, U32, tag="xo_gw")
+        xt_gs = sbuf("xt_gs", J, U8, tag="xo_gs0")
+        xt_gw = sbuf("xt_gw", J, U32, tag="xo_gw0")
         nc.vector.tensor_copy(xt_gs[:], xt_s[:].indirect(l1[:]))
         nc.vector.tensor_copy(xt_gw[:], xt_w[:].indirect(l1[:]))
         deal(w_sd, w_s, 0, PACK)
         deal(w_wd, w_w, 0, PACK)
         a = [sbuf("a%d" % t, J, F32) for t in range(PACK)]
         for t in range(PACK):
-            product(a[t], t, 0, J, w_wd, w_sd, E2M1, xt_gw, xt_gs, E4M3, False)
+            cols = slice(P * t, P * (t + 1))
+            acc = bank(J)
+            product(acc[:], w_wd[:, cols], w_sd[:, cols], E2M1, xt_gw, xt_gs, E4M3)
+            nc.vector.tensor_copy(a[t][:], acc[:])
 
-        x7_gs = sbuf("x7_gs", O, U8, tag="xo_gs")
-        x7_gw = sbuf("x7_gw", O, U32, tag="xo_gw")
+        x7_gs = sbuf("x7_gs", O, U8, tag="xo_gs0")
+        x7_gw = sbuf("x7_gw", O, U32, tag="xo_gw0")
         nc.vector.tensor_copy(x7_gs[:], xt_s[:].indirect(l7[:]))
         nc.vector.tensor_copy(x7_gw[:], xt_w[:].indirect(l7[:]))
         halves = N // P
@@ -163,31 +183,53 @@ def tile_list_ownsum_twotab_further_plain_kernel(
 
         pg = [sbuf("pg%d" % t, C, F32) for t in range(PACK)]
         hid = pool.tile([P, O, PACK], BF16, name="hid", align_bytes=64)
-        clocks = {}
+        ga = [sbuf("ga%d" % t, O, F32) for t in range(PACK)]
+        gb = [sbuf("gb%d" % t, O, F32) for t in range(PACK)]
+        diff = [pool.tile([P, 2, O], F32, name="diff%d" % u) for u in range(2)]
+        hid_w = sbuf("hid_w", O, U32)
+        hid_s = sbuf("hid_s", O, U8)
 
         def put_a(t):
             nc.scalar.activation(pw[t % 2][:].indirect(l3[:]), a[t][:], COPY)
             nc.vector.tensor_tensor(pg[t][:], pw[t % 2][:], pv[t][:], ALU.add)
 
-        def fetch(t):
-            ga = sbuf("ga%d" % t, O, F32)
-            gb = sbuf("gb%d" % t, O, F32)
-            nc.scalar.activation(ga[:], pg[t][:].indirect(l5[:]), COPY, scale=sa_t[:, t : t + 1])
-            nc.scalar.activation(gb[:], pg[t][:].indirect(l6[:]), COPY, scale=sb_t[:, t : t + 1])
-            d = sbuf("d%d" % t, O, F32)
-            nc.vector.tensor_tensor(d[:], ga[:], gb[:], ALU.subtract)
-            nc.vector.scalar_tensor_tensor(hid[:, :, t], d[:], -1.0, d[:], ALU.mult, ALU.max)
-            clocks[t] = gb
+        def fetch_a(t):
+            nc.scalar.activation(ga[t][:], pg[t][:].indirect(l5[:]), COPY, scale=sa_t[:, t : t + 1])
+
+        def fetch_b(t, o0, o1):
+            nc.scalar.activation(
+                gb[t][:, o0:o1], pg[t][:].indirect(entries(l6, o0, o1)), COPY, scale=sb_t[:, t : t + 1]
+            )
+            nc.vector.tensor_tensor(diff[t // 2][:, t % 2, o0:o1], ga[t][:, o0:o1], gb[t][:, o0:o1], ALU.subtract)
+
+        def magnitude(u, o0, o1):
+            d = diff[u][:, :, o0:o1].rearrange("p e o -> p o e")
+            nc.vector.scalar_tensor_tensor(hid[:, o0:o1, 2 * u : 2 * u + 2], d, -1.0, d, ALU.mult, ALU.max)
+
+        def quantise(o0, o1):
+            nc.vector.quantize_mx(
+                hid_w[:, o0:o1].bitcast(E4M3), hid_s[:, o0:o1], hid[:, o0:o1, :].rearrange("p o t -> p (o t)")
+            )
 
         put_a(0)
-        for t in range(1, PACK):
-            put_a(t)
-            fetch(t - 1)
-        fetch(PACK - 1)
-
-        hid_w = sbuf("hid_w", O, U32)
-        hid_s = sbuf("hid_s", O, U8)
-        nc.vector.quantize_mx(hid_w[:].bitcast(E4M3), hid_s[:], hid[:].rearrange("p o t -> p (o t)"))
+        put_a(1)
+        fetch_a(0)
+        fetch_b(0, 0, O)
+        put_a(2)
+        fetch_a(1)
+        put_a(3)
+        fetch_b(1, 0, O)
+        magnitude(0, 0, O)
+        fetch_a(2)
+        fetch_b(2, 0, O)
+        fetch_a(3)
+        pieces = ((0, O // 2), (O // 2, O))
+        for o0, o1 in pieces:
+            fetch_b(3, o0, o1)
+        for o0, o1 in pieces:
+            magnitude(1, o0, o1)
+        for o0, o1 in pieces:
+            quantise(o0, o1)
         for h in range(halves):
             cols = slice(P * h, P * (h + 1))
             nc.tensor.matmul_mx(

@@ -70,6 +70,11 @@ def tile_list_ownsum_twotab_further_plain_kernel(
         def entries(lst, j0, j1):
             return lst[:, j0 // LANES : j1 // LANES]
 
+        warm_in = sbuf("warm_in", 1, F32)
+        warm_out = sbuf("warm_out", 1, F32)
+        nc.gpsimd.memset(warm_in[:], 0.0)
+        nc.scalar.activation(warm_out[:], warm_in[:], COPY)
+
         l2 = load_list("l2", offs2)
         w2_stage = pool.tile([PACK, QUADS, R // 4], I32, name="w2_stage", tag="w2_stage", align_bytes=64)
         nc.sync.dma_start(w2_stage[:], w2_scales[0].bitcast(I32).rearrange("(q r) n -> r q n", r=PACK))

@@ -15,6 +15,7 @@ E4M3 = mybir.dt.float8_e4m3fn_x4
 E5M2 = mybir.dt.float8_e5m2_x4
 E2M1 = mybir.dt.float4_e2m1fn_x4
 COPY = mybir.ActivationFunctionType.Copy
+ABS = mybir.ActivationFunctionType.Abs
 ALU = mybir.AluOpType
 
 P = 128
@@ -61,25 +62,31 @@ def tile_list_ownsum_twotab_further_plain_kernel(
                 )
             return plane
 
-        def deal(dst, src, t0, t1):
-            nc.vector.tensor_copy(
-                dst[:].rearrange("p (t m) -> p m t", m=P),
+        def deal(dst, src, t0, t1, copy=nc.vector.tensor_copy):
+            copy(
+                dst.rearrange("p (t m) -> p m t", m=P),
                 src[:].rearrange("p (m t) -> p m t", t=PACK)[:, :, t0:t1],
             )
 
         def entries(lst, j0, j1):
             return lst[:, j0 // LANES : j1 // LANES]
 
+        xo_s = sbuf("xo_s", Z, U8)
+        nc.gpsimd.memset(xo_s[:].bitcast(I32), 0)
         warm_in = sbuf("warm_in", 1, F32)
         warm_out = sbuf("warm_out", 1, F32)
         nc.gpsimd.memset(warm_in[:], 0.0)
-        nc.scalar.activation(warm_out[:], warm_in[:], COPY)
+        nc.scalar.activation(warm_out[:], warm_in[:], ABS)
 
         l2 = load_list("l2", offs2)
         w2_stage = pool.tile([PACK, QUADS, R // 4], I32, name="w2_stage", tag="w2_stage", align_bytes=64)
         nc.sync.dma_start(w2_stage[:], w2_scales[0].bitcast(I32).rearrange("(q r) n -> r q n", r=PACK))
-        xo_s = load_scales("xo_s", xo_scales)
         xo_w = load_words("xo_w", xo_words, U16)
+        for q in range(QUADS):
+            nc.sync.dma_start(
+                xo_s[QUAD * q : QUAD * q + PACK, :].bitcast(I32),
+                xo_scales[0, PACK * q : PACK * (q + 1), :].bitcast(I32),
+            )
         w2_w = tenant("w2_w", R, U32, 0)
         nc.sync.dma_start(w2_w[:].bitcast(I32), w2_words[0].rearrange("p n t -> p (n t)").bitcast(I32))
         l4 = load_list("l4", offs4)
@@ -104,10 +111,9 @@ def tile_list_ownsum_twotab_further_plain_kernel(
         w2_s = sbuf("w2_s", R, U8)
         nc.vector.memset(w2_s[:].bitcast(I32), 0)
         pv = [sbuf("pv%d" % t, C, F32) for t in range(PACK)]
-        pw = [sbuf("pw0", C, F32)]
         for board in pv[:2]:
             nc.vector.memset(board[:], 0.0)
-        for board in pv[2:] + pw:
+        for board in pv[2:]:
             nc.gpsimd.memset(board[:], 0.0)
 
         def product(acc, words, scales, wfmt, gw, gs, gfmt):
@@ -128,9 +134,10 @@ def tile_list_ownsum_twotab_further_plain_kernel(
         xo_gs = [sbuf("xo_gs0", half, U8)]
         xo_gw = [sbuf("xo_gw0", half, U16)]
         nc.vector.tensor_copy(xo_gs[0][:], xo_s[:].indirect(entries(l2, 0, half)))
-        deal(w2_sd0, w2_s, 0, 1)
+        deal(w2_sd0[:], w2_s, 0, 1)
         nc.vector.tensor_copy(xo_gw[0][:], xo_w[:].indirect(entries(l2, 0, half)))
-        deal(w2_wd, w2_w, 0, PACK)
+        deal(w2_wd[:, 0:P], w2_w, 0, 1, nc.scalar.copy)
+        deal(w2_wd[:, P:R], w2_w, 1, PACK)
         acc = bank(half)
         product(acc[:], w2_wd[:, 0:P], w2_sd0[:], E5M2, xo_gw[0], xo_gs[0], E2M1)
         nc.scalar.activation(b[0][:, 0:half], acc[:], COPY)
@@ -145,7 +152,7 @@ def tile_list_ownsum_twotab_further_plain_kernel(
         product(acc[:], w2_wd[:, 0:P], w2_sd0[:], E5M2, xo_gw[1], xo_gs[1], E2M1)
         nc.vector.tensor_copy(b[0][:, half:J], acc[:])
         nc.scalar.activation(pv[0][:].indirect(entries(l4, half, J)), b[0][:, half:J], COPY)
-        deal(w2_sdr, w2_s, 1, PACK)
+        deal(w2_sdr[:], w2_s, 1, PACK)
         for t in range(1, PACK):
             acc = bank(J)
             for i in range(2):
@@ -156,16 +163,17 @@ def tile_list_ownsum_twotab_further_plain_kernel(
             nc.vector.tensor_copy(b[t][:], acc[:])
             nc.scalar.activation(pv[t][:].indirect(l4[:]), b[t][:], COPY)
 
-        pw.append(sbuf("pw1", C, F32, tag="xo_w"))
-        nc.vector.memset(pw[1][:], 0.0)
+        pw = [sbuf("pw0", C, F32, tag="xo_s"), sbuf("pw1", C, F32, tag="xo_w")]
+        for board in pw:
+            nc.vector.memset(board[:], 0.0)
         w_sd = tenant("w_sd", R, U8, 0)
         w_wd = sbuf("w_wd", R, U16, tag="w2_wd")
         xt_gs = sbuf("xt_gs", J, U8, tag="xo_gs0")
         xt_gw = sbuf("xt_gw", J, U32, tag="xo_gw0")
         nc.vector.tensor_copy(xt_gs[:], xt_s[:].indirect(l1[:]))
         nc.vector.tensor_copy(xt_gw[:], xt_w[:].indirect(l1[:]))
-        deal(w_sd, w_s, 0, PACK)
-        deal(w_wd, w_w, 0, PACK)
+        deal(w_sd[:], w_s, 0, PACK)
+        deal(w_wd[:], w_w, 0, PACK)
         a = [sbuf("a%d" % t, J, F32) for t in range(PACK)]
         for t in range(PACK):
             cols = slice(P * t, P * (t + 1))
@@ -209,7 +217,10 @@ def tile_list_ownsum_twotab_further_plain_kernel(
 
         def magnitude(u, o0, o1):
             d = diff[u][:, :, o0:o1].rearrange("p e o -> p o e")
-            nc.vector.scalar_tensor_tensor(hid[:, o0:o1, 2 * u : 2 * u + 2], d, -1.0, d, ALU.mult, ALU.max)
+            if u == 0:
+                nc.vector.scalar_tensor_tensor(hid[:, o0:o1, 0:2], d, -1.0, d, ALU.mult, ALU.max)
+            else:
+                nc.scalar.activation(hid[:, o0:o1, 2:4], d, ABS)
 
         def quantise(o0, o1):
             nc.vector.quantize_mx(

@@ -110,11 +110,9 @@ def tile_list_ownsum_twotab_further_plain_kernel(
 
         w2_s = sbuf("w2_s", R, U8)
         nc.vector.memset(w2_s[:].bitcast(I32), 0)
-        pv = [sbuf("pv%d" % t, C, F32) for t in range(PACK)]
-        for board in pv[:2]:
-            nc.vector.memset(board[:], 0.0)
-        for board in pv[2:]:
-            nc.gpsimd.memset(board[:], 0.0)
+        pv = [sbuf("pv0", C, F32), sbuf("pv1", C, F32)]
+        nc.vector.memset(pv[0][:], 0.0)
+        nc.gpsimd.memset(pv[1][:], 0.0)
 
         def product(acc, words, scales, wfmt, gw, gs, gfmt):
             nc.tensor.matmul_mx(
@@ -153,6 +151,8 @@ def tile_list_ownsum_twotab_further_plain_kernel(
         nc.vector.tensor_copy(b[0][:, half:J], acc[:])
         nc.scalar.activation(pv[0][:].indirect(entries(l4, half, J)), b[0][:, half:J], COPY)
         deal(w2_sdr[:], w2_s, 1, PACK)
+        pv.append(sbuf("pv2", C, F32, tag="w2_s"))
+        pv.append(tenant("pv3", C, F32, 2 * R))
         for t in range(1, PACK):
             acc = bank(J)
             for i in range(2):
@@ -161,6 +161,8 @@ def tile_list_ownsum_twotab_further_plain_kernel(
                     w2_sdr[:, P * (t - 1) : P * t], E5M2, xo_gw[i], xo_gs[i], E2M1,
                 )
             nc.vector.tensor_copy(b[t][:], acc[:])
+            if t >= 2:
+                nc.vector.memset(pv[t][:], 0.0)
             nc.scalar.activation(pv[t][:].indirect(l4[:]), b[t][:], COPY)
 
         pw = [sbuf("pw0", C, F32, tag="xo_s"), sbuf("pw1", C, F32, tag="xo_w")]

from contextlib import ExitStack

import concourse.mybir as mybir

K, T, J, R, Z, C, O, N = 512, 1024, 256, 512, 1024, 512, 128, 256
FLOPS = 2 * K * (2 * R * J + 2 * N * O)

F32 = mybir.dt.float32
BF16 = mybir.dt.bfloat16
I32 = mybir.dt.int32
U32 = mybir.dt.uint32
U16 = mybir.dt.uint16
U8 = mybir.dt.uint8
E4M3 = mybir.dt.float8_e4m3fn_x4
E5M2 = mybir.dt.float8_e5m2_x4
E2M1 = mybir.dt.float4_e2m1fn_x4
COPY = mybir.ActivationFunctionType.Copy
ABS = mybir.ActivationFunctionType.Abs
ALU = mybir.AluOpType

P = 128
PACK = 4
QUADS = 4
QUAD = 32
LANES = 16


def tile_list_ownsum_twotab_further_plain_kernel(
    tc, xt_words, xt_scales, xo_words, xo_scales, w_words, w_scales, w2_words, w2_scales, sa, sb,
    wb_words, wb_scales, ws_words, ws_scales, offs, offs2, offs3, offs4, offs5, offs6, offs7, out,
):
    nc = tc.nc
    with ExitStack() as ctx:
        pool = ctx.enter_context(tc.tile_pool(name="keep", bufs=1))
        shared = ctx.enter_context(tc.tile_pool(name="shared", bufs=1))
        psum = ctx.enter_context(tc.psum_pool(name="psum", bufs=1))

        def sbuf(name, cols, dtype, tag=None):
            return pool.tile([P, cols], dtype, name=name, tag=tag or name, align_bytes=64)

        def tenant(name, cols, dtype, offset):
            return shared.tile([P, cols], dtype, name=name, align_bytes=64, offset=offset)

        def load_list(name, src):
            t = pool.tile([P, src.shape[1]], U16, name=name)
            nc.sync.dma_start(t[:], src)
            return t

        def load_words(name, src, dtype):
            rows = src[0] if src.ndim == 3 else src[0].rearrange("p n t -> p (n t)")
            rows = rows.bitcast(I32)
            t = sbuf(name, rows.shape[1] * (2 if dtype == U16 else 1), dtype)
            nc.sync.dma_start(t[:].bitcast(I32), rows)
            return t

        def load_scales(name, src):
            plane = sbuf(name, src.shape[2], U8)
            for q in range(QUADS):
                rows = src[0, PACK * q : PACK * (q + 1), :].bitcast(I32)
                nc.sync.dma_start(
                    plane[QUAD * q : QUAD * (q + 1), :].bitcast(I32), rows.partition_broadcast(QUAD // PACK)
                )
            return plane

        def deal(dst, src, t0, t1, copy=nc.vector.tensor_copy):
            copy(
                dst.rearrange("p (t m) -> p m t", m=P),
                src[:].rearrange("p (m t) -> p m t", t=PACK)[:, :, t0:t1],
            )

        def entries(lst, j0, j1):
            return lst[:, j0 // LANES : j1 // LANES]

        xo_s = sbuf("xo_s", Z, U8)
        nc.gpsimd.memset(xo_s[:].bitcast(I32), 0)
        warm_in = sbuf("warm_in", 1, F32)
        warm_out = sbuf("warm_out", 1, F32)
        nc.gpsimd.memset(warm_in[:], 0.0)
        nc.scalar.activation(warm_out[:], warm_in[:], ABS)

        l2 = load_list("l2", offs2)
        w2_stage = pool.tile([PACK, QUADS, R // 4], I32, name="w2_stage", tag="w2_stage", align_bytes=64)
        nc.sync.dma_start(w2_stage[:], w2_scales[0].bitcast(I32).rearrange("(q r) n -> r q n", r=PACK))
        xo_w = load_words("xo_w", xo_words, U16)
        for q in range(QUADS):
            nc.sync.dma_start(
                xo_s[QUAD * q : QUAD * q + PACK, :].bitcast(I32),
                xo_scales[0, PACK * q : PACK * (q + 1), :].bitcast(I32),
            )
        w2_w = tenant("w2_w", R, U32, 0)
        nc.sync.dma_start(w2_w[:].bitcast(I32), w2_words[0].rearrange("p n t -> p (n t)").bitcast(I32))
        l4 = load_list("l4", offs4)
        l1 = load_list("l1", offs)
        xt_w = load_words("xt_w", xt_words, U32)
        xt_s = load_scales("xt_s", xt_scales)
        w_w = load_words("w_w", w_words, U16)
        w_s = load_scales("w_s", w_scales)
        l3 = load_list("l3", offs3)
        l7 = load_list("l7", offs7)
        l5 = load_list("l5", offs5)
        l6 = load_list("l6", offs6)
        sa_t = pool.tile([P, PACK], F32, name="sa_t")
        sb_t = pool.tile([P, PACK], F32, name="sb_t")
        nc.sync.dma_start(sa_t[:], sa.rearrange("(p t) o -> p (t o)", t=PACK))
        nc.sync.dma_start(sb_t[:], sb.rearrange("(p t) o -> p (t o)", t=PACK))
        ws_w = load_words("ws_w", ws_words, U32)
        ws_s = load_scales("ws_s", ws_scales)
        wb_w = load_words("wb_w", wb_words, U32)
        wb_s = load_scales("wb_s", wb_scales)

        w2_s = sbuf("w2_s", R, U8)
        nc.vector.memset(w2_s[:].bitcast(I32), 0)
        pv = [sbuf("pv0", C, F32), sbuf("pv1", C, F32)]
        nc.vector.memset(pv[0][:], 0.0)
        nc.gpsimd.memset(pv[1][:], 0.0)

        def product(acc, words, scales, wfmt, gw, gs, gfmt):
            nc.tensor.matmul_mx(
                acc, lhsT=words.bitcast(wfmt), lhsT_scale=scales,
                rhs=gw[:].bitcast(gfmt), rhs_scale=gs[:], start=True, stop=True,
            )

        def bank(cols):
            return psum.tile([P, cols], F32, name="acc", tag="acc", bufs=6)

        half = J // 2
        w2_wd = sbuf("w2_wd", R, U32)
        w2_sd0 = sbuf("w2_sd0", P, U8)
        b = [sbuf("b%d" % t, J, F32) for t in range(PACK)]
        for q in range(QUADS):
            nc.vector.tensor_copy(w2_s[QUAD * q : QUAD * q + PACK, :].bitcast(I32), w2_stage[:, q, :])
        xo_gs = [sbuf("xo_gs0", half, U8)]
        xo_gw = [sbuf("xo_gw0", half, U16)]
        nc.vector.tensor_copy(xo_gs[0][:], xo_s[:].indirect(entries(l2, 0, half)))
        deal(w2_sd0[:], w2_s, 0, 1)
        nc.vector.tensor_copy(xo_gw[0][:], xo_w[:].indirect(entries(l2, 0, half)))
        deal(w2_wd[:, 0:P], w2_w, 0, 1, nc.scalar.copy)
        deal(w2_wd[:, P:R], w2_w, 1, PACK)
        acc = bank(half)
        product(acc[:], w2_wd[:, 0:P], w2_sd0[:], E5M2, xo_gw[0], xo_gs[0], E2M1)
        nc.scalar.activation(b[0][:, 0:half], acc[:], COPY)
        nc.scalar.activation(pv[0][:].indirect(entries(l4, 0, half)), b[0][:, 0:half], COPY)

        xo_gs.append(tenant("xo_gs1", half, U8, 0))
        xo_gw.append(tenant("xo_gw1", half, U16, half))
        w2_sdr = tenant("w2_sdr", R - P, U8, 3 * half)
        nc.vector.tensor_copy(xo_gs[1][:], xo_s[:].indirect(entries(l2, half, J)))
        nc.vector.tensor_copy(xo_gw[1][:], xo_w[:].indirect(entries(l2, half, J)))
        acc = bank(half)
        product(acc[:], w2_wd[:, 0:P], w2_sd0[:], E5M2, xo_gw[1], xo_gs[1], E2M1)
        nc.vector.tensor_copy(b[0][:, half:J], acc[:])
        nc.scalar.activation(pv[0][:].indirect(entries(l4, half, J)), b[0][:, half:J], COPY)
        deal(w2_sdr[:], w2_s, 1, PACK)
        pv.append(sbuf("pv2", C, F32, tag="w2_s"))
        pv.append(tenant("pv3", C, F32, 2 * R))
        for t in range(1, PACK):
            acc = bank(J)
            for i in range(2):
                product(
                    acc[:, half * i : half * (i + 1)], w2_wd[:, P * t : P * (t + 1)],
                    w2_sdr[:, P * (t - 1) : P * t], E5M2, xo_gw[i], xo_gs[i], E2M1,
                )
            nc.vector.tensor_copy(b[t][:], acc[:])
            if t >= 2:
                nc.vector.memset(pv[t][:], 0.0)
            nc.scalar.activation(pv[t][:].indirect(l4[:]), b[t][:], COPY)

        pw = [sbuf("pw0", C, F32, tag="xo_s"), sbuf("pw1", C, F32, tag="xo_w")]
        for board in pw:
            nc.vector.memset(board[:], 0.0)
        w_sd = tenant("w_sd", R, U8, 0)
        w_wd = sbuf("w_wd", R, U16, tag="w2_wd")
        xt_gs = sbuf("xt_gs", J, U8, tag="xo_gs0")
        xt_gw = sbuf("xt_gw", J, U32, tag="xo_gw0")
        nc.vector.tensor_copy(xt_gs[:], xt_s[:].indirect(l1[:]))
        nc.vector.tensor_copy(xt_gw[:], xt_w[:].indirect(l1[:]))
        deal(w_sd[:], w_s, 0, PACK)
        deal(w_wd[:], w_w, 0, PACK)
        a = [sbuf("a%d" % t, J, F32) for t in range(PACK)]
        for t in range(PACK):
            cols = slice(P * t, P * (t + 1))
            acc = bank(J)
            product(acc[:], w_wd[:, cols], w_sd[:, cols], E2M1, xt_gw, xt_gs, E4M3)
            nc.vector.tensor_copy(a[t][:], acc[:])

        x7_gs = sbuf("x7_gs", O, U8, tag="xo_gs0")
        x7_gw = sbuf("x7_gw", O, U32, tag="xo_gw0")
        nc.vector.tensor_copy(x7_gs[:], xt_s[:].indirect(l7[:]))
        nc.vector.tensor_copy(x7_gw[:], xt_w[:].indirect(l7[:]))
        halves = N // P
        y = [psum.tile([P, O], F32, name="y%d" % h) for h in range(halves)]
        for h in range(halves):
            cols = slice(P * h, P * (h + 1))
            nc.tensor.matmul_mx(
                y[h][:], lhsT=ws_w[:, cols].bitcast(E5M2), lhsT_scale=ws_s[:, cols],
                rhs=x7_gw[:].bitcast(E4M3), rhs_scale=x7_gs[:], start=True, stop=False,
            )

        pg = [sbuf("pg%d" % t, C, F32) for t in range(PACK)]
        hid = pool.tile([P, O, PACK], BF16, name="hid", align_bytes=64)
        ga = [sbuf("ga%d" % t, O, F32) for t in range(PACK)]
        gb = [sbuf("gb%d" % t, O, F32) for t in range(PACK)]
        diff = [pool.tile([P, 2, O], F32, name="diff%d" % u) for u in range(2)]
        hid_w = sbuf("hid_w", O, U32)
        hid_s = sbuf("hid_s", O, U8)

        def put_a(t):
            nc.scalar.activation(pw[t % 2][:].indirect(l3[:]), a[t][:], COPY)
            nc.vector.tensor_tensor(pg[t][:], pw[t % 2][:], pv[t][:], ALU.add)

        def fetch_a(t):
            nc.scalar.activation(ga[t][:], pg[t][:].indirect(l5[:]), COPY, scale=sa_t[:, t : t + 1])

        def fetch_b(t, o0, o1):
            nc.scalar.activation(
                gb[t][:, o0:o1], pg[t][:].indirect(entries(l6, o0, o1)), COPY, scale=sb_t[:, t : t + 1]
            )
            nc.vector.tensor_tensor(diff[t // 2][:, t % 2, o0:o1], ga[t][:, o0:o1], gb[t][:, o0:o1], ALU.subtract)

        def magnitude(u, o0, o1):
            d = diff[u][:, :, o0:o1].rearrange("p e o -> p o e")
            if u == 0:
                nc.vector.scalar_tensor_tensor(hid[:, o0:o1, 0:2], d, -1.0, d, ALU.mult, ALU.max)
            else:
                nc.scalar.activation(hid[:, o0:o1, 2:4], d, ABS)

        def quantise(o0, o1):
            nc.vector.quantize_mx(
                hid_w[:, o0:o1].bitcast(E4M3), hid_s[:, o0:o1], hid[:, o0:o1, :].rearrange("p o t -> p (o t)")
            )

        put_a(0)
        put_a(1)
        fetch_a(0)
        fetch_b(0, 0, O)
        put_a(2)
        fetch_a(1)
        put_a(3)
        fetch_b(1, 0, O)
        magnitude(0, 0, O)
        fetch_a(2)
        fetch_b(2, 0, O)
        fetch_a(3)
        pieces = ((0, O // 2), (O // 2, O))
        for o0, o1 in pieces:
            fetch_b(3, o0, o1)
        for o0, o1 in pieces:
            magnitude(1, o0, o1)
        for o0, o1 in pieces:
            quantise(o0, o1)
        for h in range(halves):
            cols = slice(P * h, P * (h + 1))
            nc.tensor.matmul_mx(
                y[h][:], lhsT=wb_w[:, cols].bitcast(E5M2), lhsT_scale=wb_s[:, cols],
                rhs=hid_w[:].bitcast(E4M3), rhs_scale=hid_s[:], start=False, stop=True,
            )
        y0 = sbuf("y0s", O, F32)
        y1 = sbuf("y1s", O, F32)
        nc.vector.tensor_copy(y0[:], y[0][:])
        nc.sync.dma_start(out[0:P, :], y0[:])
        nc.scalar.activation(y1[:], y[1][:], COPY)
        nc.scalar.dma_start(out[P:N, :], y1[:])
